import numpy as np
import ml_dtypes


def mxq(x, axis, fmt="e4m3"):
    dtype, down = {"e4m3": (ml_dtypes.float8_e4m3fn, 7), "e5m2": (ml_dtypes.float8_e5m2, 14)}[fmt]
    v = np.moveaxis(np.asarray(x, np.float32).astype(ml_dtypes.bfloat16).astype(np.float64), axis, -1)
    blocks = v.reshape(v.shape[:-1] + (-1, 32))
    amax = np.abs(blocks).max(-1, keepdims=True)
    byte = np.maximum(np.where(amax > 0, np.frexp(amax)[1] - 1 + 127, 0) - down, 1)
    scale = np.exp2(byte - 127.0)
    codes = (blocks / scale).astype(np.float32).astype(dtype).astype(np.float64)
    return np.moveaxis((codes * scale).reshape(v.shape), -1, axis)


WIDE = False


def mx_kscale(k):
    if not WIDE:
        return np.ones(k)
    levels = np.array([10, -10, 5, -5, 0])
    if k % 512:
        return np.exp2(np.random.permutation(np.resize(levels, k // 32))).repeat(32)
    a = np.empty((k // 512, 16))
    for p in range(k // 512):
        a[p, :8] = np.random.permutation(np.resize(levels, 8))
        for g in range(8):
            far = levels[np.abs(levels - a[p, g]) >= 10]
            a[p, g + 8] = far[np.random.randint(len(far))]
    return np.exp2(a.ravel()).repeat(32)


def f64(x):
    return np.asarray(x).astype(np.float64)


def striped(idx):
    return np.tile(idx.reshape(-1, 16).T, (8, 1)).astype(np.uint16)


def unstriped(offs):
    return offs[:16].T.reshape(-1).astype(np.int64)


def striped8(idx):
    return np.concatenate([x.reshape(-1, 16).T for x in idx]).astype(np.uint16)


def runs(offs, k):
    lists = np.stack([offs[16 * r : 16 * r + 16].T.reshape(-1) for r in range(8)]).astype(np.int64)
    return lists[np.arange(k) % 512 // 64]


def pack_weight(w):
    k, n = w.shape
    w = f64(np.asarray(w, np.float32).astype(ml_dtypes.bfloat16)).reshape(k // 32, 32, n)
    amax = np.abs(w).max(1)
    byte = np.clip(np.where(amax > 0, np.frexp(amax)[1] - 1 + 127 - 7, 1), 1, 254)
    scaled = (w * np.exp2(127.0 - byte)[:, None, :]).reshape(k, n).astype(np.float32)
    words = np.ascontiguousarray(scaled.reshape(k // 512, 128, 4, n).transpose(0, 1, 3, 2)).astype(ml_dtypes.float8_e4m3fn).view(np.uint8)
    return words, np.ascontiguousarray(byte.astype(np.uint8).reshape(k // 512, 16, n))


def unpack_weight(words, scales):
    g, p, n, _ = words.shape
    vals = np.ascontiguousarray(words).view(ml_dtypes.float8_e4m3fn).astype(np.float64) * np.repeat(np.exp2(scales.astype(np.float64) - 127.0), 8, axis=1)[..., None]
    return vals.transpose(0, 1, 3, 2).reshape(g * 512, n)


def relu(v):
    return np.maximum(v, 0.0)


K, T, S, N, H = 512, 2048, 512, 512, 512


def setup_inputs():
    n = np.random.standard_normal
    s = mx_kscale(K)[:, None]
    u = mx_kscale(S)
    packed_xT = pack_weight(n((K, T)) * s)
    return {
        "x_words": packed_xT[0],
        "x_scales": packed_xT[1],
        "wa": (n((K, H)) / np.sqrt(K) / s).astype(np.float32),
        "wb": (n((K, H)) / np.sqrt(K) / s).astype(np.float32),
        "gt": (np.random.uniform(0.5, 1.5, (S, 1)) * u[:, None]).astype(np.float32),
        "w1": (n((S, N)) / np.sqrt(S) / u[:, None]).astype(np.float32),
        "offs": striped(np.random.permutation(T)[:S]),
        "two": striped(np.random.permutation(T)[:S]),
        "n1": striped8(np.stack([np.random.permutation(H) for _ in range(8)])),
        "n2": striped8(np.stack([np.random.permutation(H) for _ in range(8)])),
        "n3": striped8(np.stack([np.random.permutation(H) for _ in range(8)])),
        "n4": striped8(np.stack([np.random.permutation(H) for _ in range(8)])),
    }


def reference(x_words, x_scales, wa, wb, gt, w1, offs, two, n1, n2, n3, n4):
    xq = unpack_weight(x_words, x_scales)[:, unstriped(offs)]
    y = xq.T @ mxq(f64(wa), 0, "e4m3")
    x_two = unpack_weight(x_words, x_scales)[:, unstriped(two)]
    d = x_two.T @ mxq(f64(wb), 0, "e4m3")
    z = f64(gt) * (np.maximum(np.minimum(y - (0.5 * (y[np.arange(S)[:, None], runs(n1, S)])), d[np.arange(S)[:, None], runs(n2, S)]), d[np.arange(S)[:, None], runs(n3, S)]))
    h = mxq(f64(w1), 0, "e4m3").T @ mxq(z, 0, "e4m3")
    rl = relu(h)
    ds = np.zeros((N, H))
    ds[np.arange(N)[:, None], runs(n4, N)] = rl
    return ds - (0.5 * h)

@@ -1,0 +1,200 @@
+from contextlib import ExitStack
+
+import concourse.mybir as mybir
+
+K, T, S, N, H = 512, 2048, 512, 512, 512
+FLOPS = 2 * K * S * H * 2 + 2 * S * N * H
+
+F32 = mybir.dt.float32
+BF16 = mybir.dt.bfloat16
+I32 = mybir.dt.int32
+U32 = mybir.dt.uint32
+U16 = mybir.dt.uint16
+U8 = mybir.dt.uint8
+FP8X4 = mybir.dt.float8_e4m3fn_x4
+ALU = mybir.AluOpType
+ACT = mybir.ActivationFunctionType
+
+P = 128
+HALF = H // 2
+FUSED = False
+
+
+def tile_picked_twtclampbsend_none_p_kernel(tc, x_words, x_scales, wa, wb, gt, w1, offs, two, n1, n2, n3, n4, out):
+    nc = tc.nc
+    with ExitStack() as ctx:
+        sb = ctx.enter_context(tc.tile_pool(name="sb", bufs=1))
+        ps = ctx.enter_context(tc.psum_pool(name="ps", bufs=1))
+
+        def tile(name, shape, dtype):
+            return sb.tile(shape, dtype, name=name, align_bytes=64)
+
+        def load_list(name, src):
+            t = tile(name, [P, 32], U16)
+            nc.sync.dma_start(t[:], src)
+            return t
+
+        def load_weight(name, src):
+            t = tile(name, [P, 4, H], F32)
+            nc.sync.dma_start(t[:], src.rearrange("(p j) n -> p j n", j=4))
+            return t
+
+        xs = tile("xs", [P, T], U8)
+        l_two = load_list("l_two", two)
+        for q in range(4):
+            nc.sync.dma_start(xs[32 * q : 32 * q + 32, :].bitcast(I32), x_scales[0, 4 * q : 4 * q + 4, :].bitcast(I32).partition_broadcast(8))
+        wb_raw = load_weight("wb_raw", wb)
+        l_offs = load_list("l_offs", offs)
+        xw = tile("xw", [P, T], U32)
+        nc.sync.dma_start(xw[:].bitcast(I32), x_words[0].rearrange("p n t -> p (n t)").bitcast(I32))
+        g = tile("g", [P, 4, 1], F32)
+        with nc.allow_non_contiguous_dma(reason="one gate value a row"):
+            for e in range(4):
+                nc.gpsimd.dma_start(g[e:P:4, :, :], gt.rearrange("(c t e) o -> e c t o", t=4, e=4)[e])
+        l_n2 = load_list("l_n2", n2)
+        l_n3 = load_list("l_n3", n3)
+        wa_raw = load_weight("wa_raw", wa)
+        l_n1 = load_list("l_n1", n1)
+        w1_raw = tile("w1_raw", [P, 4, N], F32)
+        for t in range(4):
+            nc.sync.dma_start(w1_raw[:, t, :], w1.rearrange("(c t e) n -> t c e n", t=4, e=4)[t])
+        l_n4 = load_list("l_n4", n4)
+
+        twice = tile("twice", [P, 4, 1], F32)
+        sign = tile("sign", [P, 4, 1], F32)
+        mag = tile("mag", [P, 4, 1], F32)
+        nhalf = tile("nhalf", [P, 4, 1], F32)
+        nc.gpsimd.tensor_scalar(twice[:], g[:], 0.0, 2.0, ALU.is_ge, ALU.mult)
+        nc.gpsimd.tensor_scalar(sign[:], twice[:], 1.0, -1.0, ALU.mult, ALU.add)
+        nc.gpsimd.tensor_tensor(mag[:], g[:], sign[:], ALU.mult)
+        nc.gpsimd.tensor_scalar(nhalf[:], mag[:], -0.5, 0.0, ALU.mult, ALU.add)
+
+        def pick_bytes(name, lst):
+            raw = tile(name + "_raw", [P, S], U8)
+            nc.vector.tensor_copy(raw[:], xs[:].indirect(lst[:]))
+            dealt = tile(name, [P, S], U8)
+            nc.vector.tensor_copy(
+                dealt[:].bitcast(I32).rearrange("p (t c) -> p t c", t=4),
+                raw[:].bitcast(I32).rearrange("p (c t) -> p t c", t=4),
+            )
+            return dealt
+
+        def pick_words(name, lst):
+            dealt = tile(name, [P, S], U32)
+            nc.vector.tensor_copy(dealt[:].rearrange("p (t c e) -> p c t e", t=4, e=4), xw[:].indirect(lst[:]))
+            return dealt
+
+        def weave(copy, name, planes, width):
+            woven = tile(name, [P, width, 4], BF16)
+            copy(woven[:].rearrange("p (c i) t -> p c t i", i=4), planes.rearrange("p t (c i) -> p c t i", i=4))
+            return woven[:].rearrange("p c t -> p (c t)")
+
+        def quantise(woven, codes, scales):
+            nc.vector.quantize_mx(out=codes.bitcast(FP8X4), scales=scales, in_=woven)
+
+        def product(acc, lc, ls, rc, rs):
+            nc.tensor.matmul_mx(out=acc, lhsT=lc.bitcast(FP8X4), lhsT_scale=ls, rhs=rc.bitcast(FP8X4), rhs_scale=rs, start=True, stop=True)
+
+        halves = [slice(0, HALF), slice(HALF, H)]
+        lcols = [slice(0, 16), slice(16, 32)]
+        blocks = [slice(P * t, P * t + P) for t in range(4)]
+
+        two_s = pick_bytes("two_s", l_two)
+        wb_c = tile("wb_c", [P, H], U32)
+        wb_s = tile("wb_s", [P, H], U8)
+        wv0 = weave(nc.scalar.copy, "wb_w0", wb_raw[:, :, halves[0]], HALF)
+        wv1 = weave(nc.vector.tensor_copy, "wb_w1", wb_raw[:, :, halves[1]], HALF)
+        offs_s = pick_bytes("offs_s", l_offs)
+        quantise(wv1, wb_c[:, halves[1]], wb_s[:, halves[1]])
+        quantise(wv0, wb_c[:, halves[0]], wb_s[:, halves[0]])
+        two_w = pick_words("two_w", l_two)
+        offs_w = pick_words("offs_w", l_offs)
+
+        d_win = []
+        for t in range(4):
+            acc = ps.tile([P, H], F32, name="acc_d%d" % t, tag="bank%d" % t)
+            product(acc[:], two_w[:, blocks[t]], two_s[:, blocks[t]], wb_c[:], wb_s[:])
+            win = tile("d_win%d" % t, [P, H], F32)
+            nc.scalar.activation(win[:], acc[:], ACT.Copy, scale=mag[:, t, :])
+            d_win.append(win)
+        wa_w = weave(nc.scalar.copy, "wa_w", wa_raw[:], H)
+
+        lo = [tile("lo%d" % u, [P, 4, HALF], BF16) for u in range(2)]
+        hi = [tile("hi%d" % u, [P, 4, HALF], BF16) for u in range(2)]
+
+        def fetch_d(t):
+            for u in range(2):
+                nc.vector.tensor_copy(hi[u][:, t, :], d_win[t][:].indirect(l_n2[:, lcols[u]]))
+                nc.vector.tensor_copy(lo[u][:, t, :], d_win[t][:].indirect(l_n3[:, lcols[u]]))
+
+        fetch_d(0)
+        fetch_d(1)
+        wa_c = tile("wa_c", [P, H], U32)
+        wa_s = tile("wa_s", [P, H], U8)
+        quantise(wa_w, wa_c[:], wa_s[:])
+        fetch_d(2)
+        fetch_d(3)
+
+        y_acc = []
+        y_win = []
+        y_sb = []
+        for t in range(4):
+            acc = ps.tile([P, H], F32, name="acc_y%d" % t, tag="bank%d" % (4 + t))
+            product(acc[:], offs_w[:, blocks[t]], offs_s[:, blocks[t]], wa_c[:], wa_s[:])
+            win = tile("y_win%d" % t, [P, H], F32)
+            nc.scalar.activation(win[:], acc[:], ACT.Copy, scale=nhalf[:, t, :])
+            y_acc.append(acc)
+            y_win.append(win)
+            if FUSED:
+                plain = tile("y_sb%d" % t, [P, H], F32)
+                nc.scalar.activation(plain[:], acc[:], ACT.Copy, scale=mag[:, t, :])
+                y_sb.append(plain)
+
+        w1_b = tile("w1_b", [P, 4, N], BF16)
+        for j in range(4):
+            nc.scalar.activation(w1_b[:, j, :], w1_raw[:, j, :], ACT.Copy, scale=sign[:, j, :])
+        w1_w = tile("w1_w", [P, N, 4], BF16)
+        nc.scalar.copy(w1_w[:].rearrange("p (t m) j -> p m j t", t=4), w1_b[:].rearrange("p j (m t) -> p m j t", t=4))
+
+        z_w = []
+        for u in range(2):
+            a32 = tile("a32_%d" % u, [P, 4, HALF], F32)
+            a16 = tile("a16_%d" % u, [P, 4, HALF], BF16)
+            for t in range(4):
+                if FUSED:
+                    nc.vector.tensor_tensor(a32[:, t, :], y_win[t][:].indirect(l_n1[:, lcols[u]]), y_sb[t][:, halves[u]], ALU.add)
+                else:
+                    nc.vector.tensor_copy(a32[:, t, :], y_win[t][:].indirect(l_n1[:, lcols[u]]))
+            if FUSED:
+                nc.scalar.copy(a16[:], a32[:])
+            else:
+                for t in range(4):
+                    nc.vector.scalar_tensor_tensor(a16[:, t, :], y_acc[t][:, halves[u]], mag[:, t, :], a32[:, t, :], ALU.mult, ALU.add)
+            low = tile("low%d" % u, [P, 4, HALF], BF16)
+            nc.vector.tensor_tensor(low[:], a16[:], hi[u][:], ALU.min)
+            z = tile("z%d" % u, [P, 4, HALF], BF16)
+            nc.vector.tensor_tensor(z[:], low[:], lo[u][:], ALU.max)
+            z_w.append(weave(nc.scalar.copy, "z_w%d" % u, z[:], HALF))
+
+        w1_c = tile("w1_c", [P, N], U32)
+        w1_s = tile("w1_s", [P, N], U8)
+        quantise(w1_w[:].rearrange("p m j -> p (m j)"), w1_c[:], w1_s[:])
+
+        h_acc = [ps.tile([P, H], F32, name="acc_h%d" % t, tag="bank%d" % t) for t in range(4)]
+        rl = [[tile("rl%d_%d" % (t, u), [P, HALF], F32) for u in range(2)] for t in range(4)]
+        for u in range(2):
+            z_c = tile("z_c%d" % u, [P, HALF], U32)
+            z_s = tile("z_s%d" % u, [P, HALF], U8)
+            quantise(z_w[u], z_c[:], z_s[:])
+            for t in range(4):
+                product(h_acc[t][:, halves[u]], w1_c[:, blocks[t]], w1_s[:, blocks[t]], z_c[:], z_s[:])
+                nc.scalar.activation(rl[t][u][:], h_acc[t][:, halves[u]], ACT.Relu)
+
+        out_rows = out.rearrange("(p t) n -> t p n", t=4)
+        for t in range(4):
+            ds = tile("ds%d" % t, [P, H], F32)
+            for u in range(2):
+                nc.vector.tensor_copy(ds[:].indirect(l_n4[:, lcols[u]]), rl[t][u][:])
+            res = tile("res%d" % t, [P, H], F32)
+            nc.vector.scalar_tensor_tensor(res[:], h_acc[t][:], -0.5, ds[:], ALU.mult, ALU.add)
+            nc.sync.dma_start(out_rows[t], res[:])

@@ -1,6 +1,7 @@
 from contextlib import ExitStack
 
 import concourse.mybir as mybir
+from concourse.masks import make_identity
 
 K, T, S, N, H = 512, 2048, 512, 512, 512
 FLOPS = 2 * K * S * H * 2 + 2 * S * N * H
@@ -17,7 +18,8 @@ ACT = mybir.ActivationFunctionType
 
 P = 128
 HALF = H // 2
-FUSED = False
+SPLIT = 3
+ON_PE = 3
 
 
 def tile_picked_twtclampbsend_none_p_kernel(tc, x_words, x_scales, wa, wb, gt, w1, offs, two, n1, n2, n3, n4, out):
@@ -26,8 +28,8 @@ def tile_picked_twtclampbsend_none_p_kernel(tc, x_words, x_scales, wa, wb, gt, w
         sb = ctx.enter_context(tc.tile_pool(name="sb", bufs=1))
         ps = ctx.enter_context(tc.psum_pool(name="ps", bufs=1))
 
-        def tile(name, shape, dtype):
-            return sb.tile(shape, dtype, name=name, align_bytes=64)
+        def tile(name, shape, dtype, tag=None):
+            return sb.tile(shape, dtype, name=name, tag=tag or name, align_bytes=64)
 
         def load_list(name, src):
             t = tile(name, [P, 32], U16)
@@ -50,7 +52,7 @@ def tile_picked_twtclampbsend_none_p_kernel(tc, x_words, x_scales, wa, wb, gt, w
         g = tile("g", [P, 4, 1], F32)
         with nc.allow_non_contiguous_dma(reason="one gate value a row"):
             for e in range(4):
-                nc.gpsimd.dma_start(g[e:P:4, :, :], gt.rearrange("(c t e) o -> e c t o", t=4, e=4)[e])
+                nc.sync.dma_start(g[e:P:4, :, :], gt.rearrange("(c t e) o -> e c t o", t=4, e=4)[e])
         l_n2 = load_list("l_n2", n2)
         l_n3 = load_list("l_n3", n3)
         wa_raw = load_weight("wa_raw", wa)
@@ -60,13 +62,15 @@ def tile_picked_twtclampbsend_none_p_kernel(tc, x_words, x_scales, wa, wb, gt, w
             nc.sync.dma_start(w1_raw[:, t, :], w1.rearrange("(c t e) n -> t c e n", t=4, e=4)[t])
         l_n4 = load_list("l_n4", n4)
 
+        ident = tile("ident", [P, P], F32)
+        make_identity(nc, ident[:])
         twice = tile("twice", [P, 4, 1], F32)
         sign = tile("sign", [P, 4, 1], F32)
         mag = tile("mag", [P, 4, 1], F32)
         nhalf = tile("nhalf", [P, 4, 1], F32)
         nc.gpsimd.tensor_scalar(twice[:], g[:], 0.0, 2.0, ALU.is_ge, ALU.mult)
         nc.gpsimd.tensor_scalar(sign[:], twice[:], 1.0, -1.0, ALU.mult, ALU.add)
-        nc.gpsimd.tensor_tensor(mag[:], g[:], sign[:], ALU.mult)
+        nc.scalar.activation(mag[:], g[:], ACT.Abs)
         nc.gpsimd.tensor_scalar(nhalf[:], mag[:], -0.5, 0.0, ALU.mult, ALU.add)
 
         def pick_bytes(name, lst):
@@ -114,30 +118,53 @@ def tile_picked_twtclampbsend_none_p_kernel(tc, x_words, x_scales, wa, wb, gt, w
         for t in range(4):
             acc = ps.tile([P, H], F32, name="acc_d%d" % t, tag="bank%d" % t)
             product(acc[:], two_w[:, blocks[t]], two_s[:, blocks[t]], wb_c[:], wb_s[:])
-            win = tile("d_win%d" % t, [P, H], F32)
-            nc.scalar.activation(win[:], acc[:], ACT.Copy, scale=mag[:, t, :])
+            win = tile("d_win%d" % t, [P, 2 * H], F32)
+            nc.gpsimd.memset(win[:, H:], 0.0)
+            nc.scalar.activation(win[:, :H], acc[:], ACT.Copy, scale=mag[:, t, :])
             d_win.append(win)
         wa_w = weave(nc.scalar.copy, "wa_w", wa_raw[:], H)
 
-        lo = [tile("lo%d" % u, [P, 4, HALF], BF16) for u in range(2)]
-        hi = [tile("hi%d" % u, [P, 4, HALF], BF16) for u in range(2)]
-
-        def fetch_d(t):
-            for u in range(2):
-                nc.vector.tensor_copy(hi[u][:, t, :], d_win[t][:].indirect(l_n2[:, lcols[u]]))
-                nc.vector.tensor_copy(lo[u][:, t, :], d_win[t][:].indirect(l_n3[:, lcols[u]]))
-
-        fetch_d(0)
-        fetch_d(1)
+        hi = tile("hi", [P, 4, H], BF16)
+        for t in range(4):
+            nc.vector.tensor_copy(hi[:, t, :], d_win[t][:].indirect(l_n2[:]))
         wa_c = tile("wa_c", [P, H], U32)
         wa_s = tile("wa_s", [P, H], U8)
         quantise(wa_w, wa_c[:], wa_s[:])
-        fetch_d(2)
-        fetch_d(3)
+        lo = tile("lo", [P, 4, H], BF16, tag="wa_w")
+        for t in range(4):
+            nc.vector.tensor_copy(lo[:, t, :], d_win[t][:].indirect(l_n3[:]))
+
+        w1_b = tile("w1_b", [P, 4, N], BF16)
+        for j in range(4):
+            nc.scalar.activation(w1_b[:, j, :], w1_raw[:, j, :], ACT.Copy, scale=sign[:, j, :])
+        w1_w = tile("w1_w", [P, N, 4], BF16)
+
+        def weave_w1(ms):
+            nc.scalar.copy(
+                w1_w[:].rearrange("p (t m) j -> p m j t", t=4)[:, ms],
+                w1_b[:].rearrange("p j (m t) -> p m j t", t=4)[:, ms],
+            )
+
+        weave_w1(slice(0, 64))
 
         y_acc = []
         y_win = []
-        y_sb = []
+        y_sb = [[tile("y_sb%d_%d" % (u, t), [P, HALF], F32) for t in range(4)] for u in range(2)]
+        a32 = [tile("a32_%d" % u, [P, 4, HALF], F32) for u in range(2)]
+        a16 = [tile("a16_%d" % u, [P, 4, HALF], BF16) for u in range(2)]
+
+        def fetch_y(u, t):
+            nc.scalar.activation(y_sb[u][t][:], y_acc[t][:, halves[u]], ACT.Copy, scale=mag[:, t, :])
+            nc.vector.tensor_tensor(a32[u][:, t, :], y_win[t][:].indirect(l_n1[:, lcols[u]]), y_sb[u][t][:], ALU.add)
+
+        def clamp(u):
+            nc.scalar.copy(a16[u][:], a32[u][:])
+            low = tile("low%d" % u, [P, 4, HALF], BF16)
+            nc.vector.tensor_tensor(low[:], a16[u][:], hi[:, :, halves[u]], ALU.min)
+            z = tile("z%d" % u, [P, 4, HALF], BF16)
+            nc.vector.tensor_tensor(z[:], low[:], lo[:, :, halves[u]], ALU.max)
+            return z
+
         for t in range(4):
             acc = ps.tile([P, H], F32, name="acc_y%d" % t, tag="bank%d" % (4 + t))
             product(acc[:], offs_w[:, blocks[t]], offs_s[:, blocks[t]], wa_c[:], wa_s[:])
@@ -145,56 +172,53 @@ def tile_picked_twtclampbsend_none_p_kernel(tc, x_words, x_scales, wa, wb, gt, w
             nc.scalar.activation(win[:], acc[:], ACT.Copy, scale=nhalf[:, t, :])
             y_acc.append(acc)
             y_win.append(win)
-            if FUSED:
-                plain = tile("y_sb%d" % t, [P, H], F32)
-                nc.scalar.activation(plain[:], acc[:], ACT.Copy, scale=mag[:, t, :])
-                y_sb.append(plain)
-
-        w1_b = tile("w1_b", [P, 4, N], BF16)
-        for j in range(4):
-            nc.scalar.activation(w1_b[:, j, :], w1_raw[:, j, :], ACT.Copy, scale=sign[:, j, :])
-        w1_w = tile("w1_w", [P, N, 4], BF16)
-        nc.scalar.copy(w1_w[:].rearrange("p (t m) j -> p m j t", t=4), w1_b[:].rearrange("p j (m t) -> p m j t", t=4))
-
-        z_w = []
-        for u in range(2):
-            a32 = tile("a32_%d" % u, [P, 4, HALF], F32)
-            a16 = tile("a16_%d" % u, [P, 4, HALF], BF16)
-            for t in range(4):
-                if FUSED:
-                    nc.vector.tensor_tensor(a32[:, t, :], y_win[t][:].indirect(l_n1[:, lcols[u]]), y_sb[t][:, halves[u]], ALU.add)
-                else:
-                    nc.vector.tensor_copy(a32[:, t, :], y_win[t][:].indirect(l_n1[:, lcols[u]]))
-            if FUSED:
-                nc.scalar.copy(a16[:], a32[:])
-            else:
-                for t in range(4):
-                    nc.vector.scalar_tensor_tensor(a16[:, t, :], y_acc[t][:, halves[u]], mag[:, t, :], a32[:, t, :], ALU.mult, ALU.add)
-            low = tile("low%d" % u, [P, 4, HALF], BF16)
-            nc.vector.tensor_tensor(low[:], a16[:], hi[u][:], ALU.min)
-            z = tile("z%d" % u, [P, 4, HALF], BF16)
-            nc.vector.tensor_tensor(z[:], low[:], lo[u][:], ALU.max)
-            z_w.append(weave(nc.scalar.copy, "z_w%d" % u, z[:], HALF))
-
+            fetch_y(0, t)
+        fetch_y(1, 0)
+        fetch_y(1, 1)
+        weave_w1(slice(64, 128))
+        z0 = clamp(0)
+        fetch_y(1, 2)
+        fetch_y(1, 3)
+        z_w = [weave(nc.scalar.copy, "z_w0", z0[:], HALF)]
         w1_c = tile("w1_c", [P, N], U32)
         w1_s = tile("w1_s", [P, N], U8)
         quantise(w1_w[:].rearrange("p m j -> p (m j)"), w1_c[:], w1_s[:])
+        z1 = clamp(1)
+        z_w.append(weave(nc.scalar.copy, "z_w1", z1[:], HALF))
 
         h_acc = [ps.tile([P, H], F32, name="acc_h%d" % t, tag="bank%d" % t) for t in range(4)]
-        rl = [[tile("rl%d_%d" % (t, u), [P, HALF], F32) for u in range(2)] for t in range(4)]
+        rl = [tile("rl%d" % t, [P, H], F32, tag="z1" if t == 2 else None) for t in range(4)]
         for u in range(2):
             z_c = tile("z_c%d" % u, [P, HALF], U32)
             z_s = tile("z_s%d" % u, [P, HALF], U8)
             quantise(z_w[u], z_c[:], z_s[:])
             for t in range(4):
                 product(h_acc[t][:, halves[u]], w1_c[:, blocks[t]], w1_s[:, blocks[t]], z_c[:], z_s[:])
-                nc.scalar.activation(rl[t][u][:], h_acc[t][:, halves[u]], ACT.Relu)
+                nc.scalar.activation(rl[t][:, halves[u]], h_acc[t][:, halves[u]], ACT.Relu)
 
         out_rows = out.rearrange("(p t) n -> t p n", t=4)
         for t in range(4):
-            ds = tile("ds%d" % t, [P, H], F32)
-            for u in range(2):
-                nc.vector.tensor_copy(ds[:].indirect(l_n4[:, lcols[u]]), rl[t][u][:])
+            if t < SPLIT:
+                ds = tile("ds%d" % t, [P, H], F32)
+                for u in range(2):
+                    nc.vector.tensor_copy(ds[:].indirect(l_n4[:, lcols[u]]), rl[t][:, halves[u]])
+            else:
+                ds = tile("ds%d" % t, [P, 2 * H], F32)
+                nc.vector.tensor_copy(ds[:].indirect(l_n4[:]), rl[t][:])
             res = tile("res%d" % t, [P, H], F32)
-            nc.vector.scalar_tensor_tensor(res[:], h_acc[t][:], -0.5, ds[:], ALU.mult, ALU.add)
+            if t < ON_PE:
+                nh = tile("nh%d" % t, [P, H], F32)
+                nc.scalar.activation(nh[:], h_acc[t][:], ACT.Copy, scale=-0.5)
+                turned = ps.tile([P, H], F32, name="turned%d" % t, tag="bank%d" % (4 + t % 2))
+                for b in blocks:
+                    nc.tensor.matmul(turned[:, b], nh[:, b], ident[:], start=True, stop=False, is_transpose=True)
+                    nc.tensor.matmul(turned[:, b], ds[:, b], ident[:], start=False, stop=True, is_transpose=True)
+                turned_sb = tile("turned_sb%d" % t, [P, H], F32)
+                nc.scalar.copy(turned_sb[:], turned[:])
+                back = ps.tile([P, H], F32, name="back%d" % t, tag="bank%d" % (6 + t % 2))
+                for b in blocks:
+                    nc.tensor.transpose(back[:, b], turned_sb[:, b], ident[:])
+                nc.scalar.copy(res[:], back[:])
+            else:
+                nc.vector.scalar_tensor_tensor(res[:], h_acc[t][:], -0.5, ds[:, :H], ALU.mult, ALU.add)
             nc.sync.dma_start(out_rows[t], res[:])

@@ -49,10 +49,12 @@ def tile_picked_twtclampbsend_none_p_kernel(tc, x_words, x_scales, wa, wb, gt, w
         l_offs = load_list("l_offs", offs)
         xw = tile("xw", [P, T], U32)
         nc.sync.dma_start(xw[:].bitcast(I32), x_words[0].rearrange("p n t -> p (n t)").bitcast(I32))
-        g = tile("g", [P, 4, 1], F32)
-        with nc.allow_non_contiguous_dma(reason="one gate value a row"):
-            for e in range(4):
-                nc.sync.dma_start(g[e:P:4, :, :], gt.rearrange("(c t e) o -> e c t o", t=4, e=4)[e])
+        g_rows = tile("g_rows", [P, P], F32)
+        nc.gpsimd.memset(g_rows[:], 0.0)
+        nc.gpsimd.dma_start(
+            g_rows[0:4, :].rearrange("t (c e) -> t c e", e=4),
+            gt.rearrange("(c t e) o -> t c (e o)", t=4, e=4),
+        )
         l_n2 = load_list("l_n2", n2)
         l_n3 = load_list("l_n3", n3)
         wa_raw = load_weight("wa_raw", wa)
@@ -64,10 +66,14 @@ def tile_picked_twtclampbsend_none_p_kernel(tc, x_words, x_scales, wa, wb, gt, w
 
         ident = tile("ident", [P, P], F32)
         make_identity(nc, ident[:])
-        twice = tile("twice", [P, 4, 1], F32)
-        sign = tile("sign", [P, 4, 1], F32)
-        mag = tile("mag", [P, 4, 1], F32)
-        nhalf = tile("nhalf", [P, 4, 1], F32)
+        g_ps = ps.tile([P, P], F32, name="g_ps", tag="bank7")
+        nc.tensor.transpose(g_ps[:], g_rows[:], ident[:])
+        g = tile("g", [P, 4], F32)
+        nc.scalar.copy(g[:], g_ps[:, 0:4])
+        twice = tile("twice", [P, 4], F32)
+        sign = tile("sign", [P, 4], F32)
+        mag = tile("mag", [P, 4], F32)
+        nhalf = tile("nhalf", [P, 4], F32)
         nc.gpsimd.tensor_scalar(twice[:], g[:], 0.0, 2.0, ALU.is_ge, ALU.mult)
         nc.gpsimd.tensor_scalar(sign[:], twice[:], 1.0, -1.0, ALU.mult, ALU.add)
         nc.scalar.activation(mag[:], g[:], ACT.Abs)
@@ -120,7 +126,7 @@ def tile_picked_twtclampbsend_none_p_kernel(tc, x_words, x_scales, wa, wb, gt, w
             product(acc[:], two_w[:, blocks[t]], two_s[:, blocks[t]], wb_c[:], wb_s[:])
             win = tile("d_win%d" % t, [P, 2 * H], F32)
             nc.gpsimd.memset(win[:, H:], 0.0)
-            nc.scalar.activation(win[:, :H], acc[:], ACT.Copy, scale=mag[:, t, :])
+            nc.scalar.activation(win[:, :H], acc[:], ACT.Copy, scale=mag[:, t : t + 1])
             d_win.append(win)
         wa_w = weave(nc.scalar.copy, "wa_w", wa_raw[:], H)
 
@@ -136,67 +142,72 @@ def tile_picked_twtclampbsend_none_p_kernel(tc, x_words, x_scales, wa, wb, gt, w
 
         w1_b = tile("w1_b", [P, 4, N], BF16)
         for j in range(4):
-            nc.scalar.activation(w1_b[:, j, :], w1_raw[:, j, :], ACT.Copy, scale=sign[:, j, :])
+            nc.scalar.activation(
+                w1_b[:, j, :].rearrange("p (t c e) -> p t c e", t=4, e=4),
+                w1_raw[:, j, :].rearrange("p (c t e) -> p t c e", t=4, e=4),
+                ACT.Copy,
+                scale=sign[:, j : j + 1],
+            )
         w1_w = tile("w1_w", [P, N, 4], BF16)
 
         def weave_w1(ms):
             nc.scalar.copy(
-                w1_w[:].rearrange("p (t m) j -> p m j t", t=4)[:, ms],
-                w1_b[:].rearrange("p j (m t) -> p m j t", t=4)[:, ms],
+                w1_w[:, ms, :].rearrange("p (c i) j -> p c j i", i=4),
+                w1_b[:, :, ms].rearrange("p j (c i) -> p c j i", i=4),
             )
 
-        weave_w1(slice(0, 64))
+        weave_w1(halves[0])
 
         y_acc = []
         y_win = []
         y_sb = [[tile("y_sb%d_%d" % (u, t), [P, HALF], F32) for t in range(4)] for u in range(2)]
         a32 = [tile("a32_%d" % u, [P, 4, HALF], F32) for u in range(2)]
-        a16 = [tile("a16_%d" % u, [P, 4, HALF], BF16) for u in range(2)]
 
         def fetch_y(u, t):
-            nc.scalar.activation(y_sb[u][t][:], y_acc[t][:, halves[u]], ACT.Copy, scale=mag[:, t, :])
+            nc.scalar.activation(y_sb[u][t][:], y_acc[t][:, halves[u]], ACT.Copy, scale=mag[:, t : t + 1])
             nc.vector.tensor_tensor(a32[u][:, t, :], y_win[t][:].indirect(l_n1[:, lcols[u]]), y_sb[u][t][:], ALU.add)
-
-        def clamp(u):
-            nc.scalar.copy(a16[u][:], a32[u][:])
-            low = tile("low%d" % u, [P, 4, HALF], BF16)
-            nc.vector.tensor_tensor(low[:], a16[u][:], hi[:, :, halves[u]], ALU.min)
-            z = tile("z%d" % u, [P, 4, HALF], BF16)
-            nc.vector.tensor_tensor(z[:], low[:], lo[:, :, halves[u]], ALU.max)
-            return z
 
         for t in range(4):
             acc = ps.tile([P, H], F32, name="acc_y%d" % t, tag="bank%d" % (4 + t))
             product(acc[:], offs_w[:, blocks[t]], offs_s[:, blocks[t]], wa_c[:], wa_s[:])
             win = tile("y_win%d" % t, [P, H], F32)
-            nc.scalar.activation(win[:], acc[:], ACT.Copy, scale=nhalf[:, t, :])
+            nc.scalar.activation(win[:], acc[:], ACT.Copy, scale=nhalf[:, t : t + 1])
             y_acc.append(acc)
             y_win.append(win)
             fetch_y(0, t)
         fetch_y(1, 0)
         fetch_y(1, 1)
-        weave_w1(slice(64, 128))
-        z0 = clamp(0)
+        a16 = tile("a16", [P, 4, HALF], BF16)
+        nc.scalar.copy(a16[:], a32[0][:])
+        low0 = tile("low0", [P, 4, HALF], BF16)
+        nc.vector.tensor_tensor(low0[:], a16[:], hi[:, :, halves[0]], ALU.min)
         fetch_y(1, 2)
+        z0 = tile("z0", [P, 4, HALF], BF16)
+        nc.vector.tensor_tensor(z0[:], low0[:], lo[:, :, halves[0]], ALU.max)
         fetch_y(1, 3)
-        z_w = [weave(nc.scalar.copy, "z_w0", z0[:], HALF)]
+        weave_w1(halves[1])
+        z_w0 = weave(nc.scalar.copy, "z_w0", z0[:], HALF)
         w1_c = tile("w1_c", [P, N], U32)
         w1_s = tile("w1_s", [P, N], U8)
         quantise(w1_w[:].rearrange("p m j -> p (m j)"), w1_c[:], w1_s[:])
-        z1 = clamp(1)
-        z_w.append(weave(nc.scalar.copy, "z_w1", z1[:], HALF))
+        low1 = tile("low1", [P, 4, HALF], BF16)
+        nc.vector.tensor_tensor(low1[:], a32[1][:], hi[:, :, halves[1]], ALU.min)
+        z_c = [tile("z_c%d" % u, [P, HALF], U32) for u in range(2)]
+        z_s = [tile("z_s%d" % u, [P, HALF], U8) for u in range(2)]
+        quantise(z_w0, z_c[0][:], z_s[0][:])
+        z1 = tile("z1", [P, 4, HALF], BF16, tag="z_w0")
+        nc.vector.tensor_tensor(z1[:], low1[:], lo[:, :, halves[1]], ALU.max)
+        z_w1 = weave(nc.scalar.copy, "z_w1", z1[:], HALF)
+        quantise(z_w1, z_c[1][:], z_s[1][:])
 
         h_acc = [ps.tile([P, H], F32, name="acc_h%d" % t, tag="bank%d" % t) for t in range(4)]
-        rl = [tile("rl%d" % t, [P, H], F32, tag="z1" if t == 2 else None) for t in range(4)]
+        rl = [tile("rl%d" % t, [P, H], F32, tag="z_w0" if t == 2 else None) for t in range(4)]
         for u in range(2):
-            z_c = tile("z_c%d" % u, [P, HALF], U32)
-            z_s = tile("z_s%d" % u, [P, HALF], U8)
-            quantise(z_w[u], z_c[:], z_s[:])
             for t in range(4):
-                product(h_acc[t][:, halves[u]], w1_c[:, blocks[t]], w1_s[:, blocks[t]], z_c[:], z_s[:])
+                product(h_acc[t][:, halves[u]], w1_c[:, blocks[t]], w1_s[:, blocks[t]], z_c[u][:], z_s[u][:])
                 nc.scalar.activation(rl[t][:, halves[u]], h_acc[t][:, halves[u]], ACT.Relu)
 
-        out_rows = out.rearrange("(p t) n -> t p n", t=4)
+        out_rows = out.rearrange("(c t e) n -> t c e n", t=4, e=4)
         for t in range(4):
             if t < SPLIT:
                 ds = tile("ds%d" % t, [P, H], F32)
@@ -209,16 +220,18 @@ def tile_picked_twtclampbsend_none_p_kernel(tc, x_words, x_scales, wa, wb, gt, w
             if t < ON_PE:
                 nh = tile("nh%d" % t, [P, H], F32)
                 nc.scalar.activation(nh[:], h_acc[t][:], ACT.Copy, scale=-0.5)
-                turned = ps.tile([P, H], F32, name="turned%d" % t, tag="bank%d" % (4 + t % 2))
-                for b in blocks:
-                    nc.tensor.matmul(turned[:, b], nh[:, b], ident[:], start=True, stop=False, is_transpose=True)
-                    nc.tensor.matmul(turned[:, b], ds[:, b], ident[:], start=False, stop=True, is_transpose=True)
-                turned_sb = tile("turned_sb%d" % t, [P, H], F32)
-                nc.scalar.copy(turned_sb[:], turned[:])
-                back = ps.tile([P, H], F32, name="back%d" % t, tag="bank%d" % (6 + t % 2))
-                for b in blocks:
-                    nc.tensor.transpose(back[:, b], turned_sb[:, b], ident[:])
-                nc.scalar.copy(res[:], back[:])
+                for u in range(2):
+                    turned = ps.tile([P, HALF], F32, name="turned%d_%d" % (t, u), tag="bank%d" % (4 + u))
+                    for k in range(2):
+                        b = blocks[2 * u + k]
+                        nc.tensor.matmul(turned[:, blocks[k]], nh[:, b], ident[:], start=True, stop=False, is_transpose=True)
+                        nc.tensor.matmul(turned[:, blocks[k]], ds[:, b], ident[:], start=False, stop=True, is_transpose=True)
+                    turned_sb = tile("turned_sb%d_%d" % (t, u), [P, HALF], F32)
+                    nc.scalar.copy(turned_sb[:], turned[:])
+                    back = ps.tile([P, HALF], F32, name="back%d_%d" % (t, u), tag="bank%d" % (6 + u))
+                    for k in range(2):
+                        nc.tensor.transpose(back[:, blocks[k]], turned_sb[:, blocks[k]], ident[:])
+                    nc.scalar.copy(res[:, halves[u]], back[:])
             else:
                 nc.vector.scalar_tensor_tensor(res[:], h_acc[t][:], -0.5, ds[:, :H], ALU.mult, ALU.add)
             nc.sync.dma_start(out_rows[t], res[:])

@@ -45,16 +45,15 @@ def tile_picked_twtclampbsend_none_p_kernel(tc, x_words, x_scales, wa, wb, gt, w
         l_two = load_list("l_two", two)
         for q in range(4):
             nc.sync.dma_start(xs[32 * q : 32 * q + 32, :].bitcast(I32), x_scales[0, 4 * q : 4 * q + 4, :].bitcast(I32).partition_broadcast(8))
-        wb_raw = load_weight("wb_raw", wb)
+        g16 = tile("g16", [P, 4, 4], F32)
+        nc.sync.dma_start(
+            g16[:].rearrange("p t e -> p (t e)"),
+            gt.rearrange("(c k) o -> c o k", k=16).broadcast_to([32, 4, 16]),
+        )
         l_offs = load_list("l_offs", offs)
+        wb_raw = load_weight("wb_raw", wb)
         xw = tile("xw", [P, T], U32)
         nc.sync.dma_start(xw[:].bitcast(I32), x_words[0].rearrange("p n t -> p (n t)").bitcast(I32))
-        g_rows = tile("g_rows", [P, P], F32)
-        nc.gpsimd.memset(g_rows[:], 0.0)
-        nc.gpsimd.dma_start(
-            g_rows[0:4, :].rearrange("t (c e) -> t c e", e=4),
-            gt.rearrange("(c t e) o -> t c (e o)", t=4, e=4),
-        )
         l_n2 = load_list("l_n2", n2)
         l_n3 = load_list("l_n3", n3)
         wa_raw = load_weight("wa_raw", wa)
@@ -66,10 +65,14 @@ def tile_picked_twtclampbsend_none_p_kernel(tc, x_words, x_scales, wa, wb, gt, w
 
         ident = tile("ident", [P, P], F32)
         make_identity(nc, ident[:])
-        g_ps = ps.tile([P, P], F32, name="g_ps", tag="bank7")
-        nc.tensor.transpose(g_ps[:], g_rows[:], ident[:])
+        own = tile("own", [P, 4], F32)
+        nc.vector.tensor_reduce(own[:], ident[:].rearrange("p (c e) -> p e c", e=4), mybir.AxisListType.X, ALU.add)
+        g_masked = tile("g_masked", [P, 4, 4], F32)
+        nc.gpsimd.tensor_tensor(g_masked[:], g16[:], own[:].unsqueeze(1).broadcast_to([P, 4, 4]), ALU.mult)
+        g_pairs = tile("g_pairs", [P, 4, 2], F32)
+        nc.gpsimd.tensor_tensor(g_pairs[:], g_masked[:, :, 0:2], g_masked[:, :, 2:4], ALU.add)
         g = tile("g", [P, 4], F32)
-        nc.scalar.copy(g[:], g_ps[:, 0:4])
+        nc.gpsimd.tensor_tensor(g[:], g_pairs[:, :, 0], g_pairs[:, :, 1], ALU.add)
         twice = tile("twice", [P, 4], F32)
         sign = tile("sign", [P, 4], F32)
         mag = tile("mag", [P, 4], F32)
@@ -77,7 +80,7 @@ def tile_picked_twtclampbsend_none_p_kernel(tc, x_words, x_scales, wa, wb, gt, w
         nc.gpsimd.tensor_scalar(twice[:], g[:], 0.0, 2.0, ALU.is_ge, ALU.mult)
         nc.gpsimd.tensor_scalar(sign[:], twice[:], 1.0, -1.0, ALU.mult, ALU.add)
         nc.scalar.activation(mag[:], g[:], ACT.Abs)
-        nc.gpsimd.tensor_scalar(nhalf[:], mag[:], -0.5, 0.0, ALU.mult, ALU.add)
+        nc.scalar.activation(nhalf[:], mag[:], ACT.Copy, scale=-0.5)
 
         def pick_bytes(name, lst):
             raw = tile(name + "_raw", [P, S], U8)
@@ -191,7 +194,9 @@ def tile_picked_twtclampbsend_none_p_kernel(tc, x_words, x_scales, wa, wb, gt, w
         w1_s = tile("w1_s", [P, N], U8)
         quantise(w1_w[:].rearrange("p m j -> p (m j)"), w1_c[:], w1_s[:])
         low1 = tile("low1", [P, 4, HALF], BF16)
-        nc.vector.tensor_tensor(low1[:], a32[1][:], hi[:, :, halves[1]], ALU.min)
+        b16 = tile("b16", [P, 4, HALF], BF16)
+        nc.scalar.copy(b16[:], a32[1][:])
+        nc.vector.tensor_tensor(low1[:], b16[:], hi[:, :, halves[1]], ALU.min)
         z_c = [tile("z_c%d" % u, [P, HALF], U32) for u in range(2)]
         z_s = [tile("z_s%d" % u, [P, HALF], U8) for u in range(2)]
         quantise(z_w0, z_c[0][:], z_s[0][:])

@@ -4,7 +4,7 @@ import concourse.mybir as mybir
 from concourse.masks import make_identity
 
 K, T, S, N, H = 512, 2048, 512, 512, 512
-FLOPS = 2 * K * S * H * 2 + 2 * S * N * H
+FLOPS = 2 * (2 * K * S * H) + 2 * S * N * H
 
 F32 = mybir.dt.float32
 BF16 = mybir.dt.bfloat16
@@ -17,12 +17,17 @@ ALU = mybir.AluOpType
 ACT = mybir.ActivationFunctionType
 
 P = 128
+SLOTS = 4
+RUN = 4
+LIST_COLS = S // 16
 HALF = H // 2
-SPLIT = 3
-ON_PE = 3
+QUADRANT = 32
+LAST = SLOTS - 1
 
 
-def tile_picked_twtclampbsend_none_p_kernel(tc, x_words, x_scales, wa, wb, gt, w1, offs, two, n1, n2, n3, n4, out):
+def tile_picked_twtclampbsend_none_p_kernel(
+    tc, x_words, x_scales, wa, wb, gt, w1, offs, two, n1, n2, n3, n4, out
+):
     nc = tc.nc
     with ExitStack() as ctx:
         sb = ctx.enter_context(tc.tile_pool(name="sb", bufs=1))
@@ -31,212 +36,222 @@ def tile_picked_twtclampbsend_none_p_kernel(tc, x_words, x_scales, wa, wb, gt, w
         def tile(name, shape, dtype, tag=None):
             return sb.tile(shape, dtype, name=name, tag=tag or name, align_bytes=64)
 
+        def bank(name, width, number):
+            return ps.tile([P, width], F32, name=name, tag="bank%d" % number)
+
         def load_list(name, src):
-            t = tile(name, [P, 32], U16)
-            nc.sync.dma_start(t[:], src)
-            return t
+            lst = tile(name, [P, LIST_COLS], U16)
+            nc.sync.dma_start(lst[:], src)
+            return lst
 
         def load_weight(name, src):
-            t = tile(name, [P, 4, H], F32)
-            nc.sync.dma_start(t[:], src.rearrange("(p j) n -> p j n", j=4))
-            return t
+            raw = tile(name, [P, SLOTS, H], F32)
+            nc.sync.dma_start(raw[:], src.rearrange("(p r) n -> p r n", r=SLOTS))
+            return raw
+
+        halves = [slice(0, HALF), slice(HALF, H)]
+        list_halves = [slice(0, LIST_COLS // 2), slice(LIST_COLS // 2, LIST_COLS)]
+        blocks = [slice(P * t, P * t + P) for t in range(SLOTS)]
 
         xs = tile("xs", [P, T], U8)
         l_two = load_list("l_two", two)
-        for q in range(4):
-            nc.sync.dma_start(xs[32 * q : 32 * q + 32, :].bitcast(I32), x_scales[0, 4 * q : 4 * q + 4, :].bitcast(I32).partition_broadcast(8))
-        g16 = tile("g16", [P, 4, 4], F32)
-        nc.sync.dma_start(
-            g16[:].rearrange("p t e -> p (t e)"),
-            gt.rearrange("(c k) o -> c o k", k=16).broadcast_to([32, 4, 16]),
-        )
-        l_offs = load_list("l_offs", offs)
+        for q in range(P // QUADRANT):
+            nc.sync.dma_start(
+                xs[QUADRANT * q : QUADRANT * (q + 1), :].bitcast(I32),
+                x_scales[0, 4 * q : 4 * q + 4, :].bitcast(I32).partition_broadcast(QUADRANT // 4),
+            )
         wb_raw = load_weight("wb_raw", wb)
+        l_offs = load_list("l_offs", offs)
         xw = tile("xw", [P, T], U32)
-        nc.sync.dma_start(xw[:].bitcast(I32), x_words[0].rearrange("p n t -> p (n t)").bitcast(I32))
+        nc.sync.dma_start(xw[:].bitcast(I32), x_words[0].rearrange("p n r -> p (n r)").bitcast(I32))
+        gate = tile("gate", [P, SLOTS], F32)
+        with nc.allow_non_contiguous_dma(reason="one gate value a row"):
+            for e in range(RUN):
+                nc.sync.dma_start(gate[e:P:RUN, :], gt.rearrange("(c t e) o -> e c (t o)", t=SLOTS, e=RUN)[e])
         l_n2 = load_list("l_n2", n2)
         l_n3 = load_list("l_n3", n3)
         wa_raw = load_weight("wa_raw", wa)
         l_n1 = load_list("l_n1", n1)
-        w1_raw = tile("w1_raw", [P, 4, N], F32)
-        for t in range(4):
-            nc.sync.dma_start(w1_raw[:, t, :], w1.rearrange("(c t e) n -> t c e n", t=4, e=4)[t])
+        w1_raw = tile("w1_raw", [P, SLOTS, N], F32)
+        for t in range(SLOTS):
+            nc.sync.dma_start(w1_raw[:, t, :], w1.rearrange("(c t e) n -> t c e n", t=SLOTS, e=RUN)[t])
         l_n4 = load_list("l_n4", n4)
 
         ident = tile("ident", [P, P], F32)
         make_identity(nc, ident[:])
-        own = tile("own", [P, 4], F32)
-        nc.vector.tensor_reduce(own[:], ident[:].rearrange("p (c e) -> p e c", e=4), mybir.AxisListType.X, ALU.add)
-        g_masked = tile("g_masked", [P, 4, 4], F32)
-        nc.gpsimd.tensor_tensor(g_masked[:], g16[:], own[:].unsqueeze(1).broadcast_to([P, 4, 4]), ALU.mult)
-        g_pairs = tile("g_pairs", [P, 4, 2], F32)
-        nc.gpsimd.tensor_tensor(g_pairs[:], g_masked[:, :, 0:2], g_masked[:, :, 2:4], ALU.add)
-        g = tile("g", [P, 4], F32)
-        nc.gpsimd.tensor_tensor(g[:], g_pairs[:, :, 0], g_pairs[:, :, 1], ALU.add)
-        twice = tile("twice", [P, 4], F32)
-        sign = tile("sign", [P, 4], F32)
-        mag = tile("mag", [P, 4], F32)
-        nhalf = tile("nhalf", [P, 4], F32)
-        nc.gpsimd.tensor_scalar(twice[:], g[:], 0.0, 2.0, ALU.is_ge, ALU.mult)
+        twice = tile("twice", [P, SLOTS], F32)
+        sign = tile("sign", [P, SLOTS], F32)
+        mag = tile("mag", [P, SLOTS], F32)
+        neg_half_mag = tile("neg_half_mag", [P, SLOTS], F32)
+        nc.gpsimd.tensor_scalar(twice[:], gate[:], 0.0, 2.0, ALU.is_ge, ALU.mult)
         nc.gpsimd.tensor_scalar(sign[:], twice[:], 1.0, -1.0, ALU.mult, ALU.add)
-        nc.scalar.activation(mag[:], g[:], ACT.Abs)
-        nc.scalar.activation(nhalf[:], mag[:], ACT.Copy, scale=-0.5)
+        nc.scalar.activation(mag[:], gate[:], ACT.Abs)
+        nc.scalar.activation(neg_half_mag[:], mag[:], ACT.Copy, scale=-0.5)
 
         def pick_bytes(name, lst):
-            raw = tile(name + "_raw", [P, S], U8)
-            nc.vector.tensor_copy(raw[:], xs[:].indirect(lst[:]))
+            picked = tile(name + "_picked", [P, S], U8)
+            nc.vector.tensor_copy(picked[:], xs[:].indirect(lst[:]))
             dealt = tile(name, [P, S], U8)
             nc.vector.tensor_copy(
-                dealt[:].bitcast(I32).rearrange("p (t c) -> p t c", t=4),
-                raw[:].bitcast(I32).rearrange("p (c t) -> p t c", t=4),
+                dealt[:].bitcast(I32).rearrange("p (t c) -> p t c", t=SLOTS),
+                picked[:].bitcast(I32).rearrange("p (c t) -> p t c", t=SLOTS),
             )
             return dealt
 
         def pick_words(name, lst):
             dealt = tile(name, [P, S], U32)
-            nc.vector.tensor_copy(dealt[:].rearrange("p (t c e) -> p c t e", t=4, e=4), xw[:].indirect(lst[:]))
+            nc.vector.tensor_copy(dealt[:].rearrange("p (t c e) -> p c t e", t=SLOTS, e=RUN), xw[:].indirect(lst[:]))
             return dealt
 
-        def weave(copy, name, planes, width):
-            woven = tile(name, [P, width, 4], BF16)
-            copy(woven[:].rearrange("p (c i) t -> p c t i", i=4), planes.rearrange("p t (c i) -> p c t i", i=4))
-            return woven[:].rearrange("p c t -> p (c t)")
+        def weave(copy, woven, planes):
+            copy(woven.rearrange("p (a i) r -> p a r i", i=4), planes.rearrange("p r (a i) -> p a r i", i=4))
 
-        def quantise(woven, codes, scales):
-            nc.vector.quantize_mx(out=codes.bitcast(FP8X4), scales=scales, in_=woven)
+        def mx_tiles(name, width):
+            return tile(name + "_codes", [P, width], U32), tile(name + "_scales", [P, width], U8)
 
-        def product(acc, lc, ls, rc, rs):
-            nc.tensor.matmul_mx(out=acc, lhsT=lc.bitcast(FP8X4), lhsT_scale=ls, rhs=rc.bitcast(FP8X4), rhs_scale=rs, start=True, stop=True)
+        def quantise_into(operand, cols, woven):
+            nc.vector.quantize_mx(
+                out=operand[0][:, cols].bitcast(FP8X4),
+                scales=operand[1][:, cols],
+                in_=woven[:].rearrange("p n r -> p (n r)"),
+            )
 
-        halves = [slice(0, HALF), slice(HALF, H)]
-        lcols = [slice(0, 16), slice(16, 32)]
-        blocks = [slice(P * t, P * t + P) for t in range(4)]
+        def quantise(name, woven, width):
+            operand = mx_tiles(name, width)
+            quantise_into(operand, slice(0, width), woven)
+            return operand
 
-        two_s = pick_bytes("two_s", l_two)
-        wb_c = tile("wb_c", [P, H], U32)
-        wb_s = tile("wb_s", [P, H], U8)
-        wv0 = weave(nc.scalar.copy, "wb_w0", wb_raw[:, :, halves[0]], HALF)
-        wv1 = weave(nc.vector.tensor_copy, "wb_w1", wb_raw[:, :, halves[1]], HALF)
-        offs_s = pick_bytes("offs_s", l_offs)
-        quantise(wv1, wb_c[:, halves[1]], wb_s[:, halves[1]])
-        quantise(wv0, wb_c[:, halves[0]], wb_s[:, halves[0]])
-        two_w = pick_words("two_w", l_two)
-        offs_w = pick_words("offs_w", l_offs)
+        def product(acc, stationary, t, moving):
+            nc.tensor.matmul_mx(
+                out=acc,
+                lhsT=stationary[0][:, blocks[t]].bitcast(FP8X4),
+                lhsT_scale=stationary[1][:, blocks[t]],
+                rhs=moving[0][:].bitcast(FP8X4),
+                rhs_scale=moving[1][:],
+                start=True,
+                stop=True,
+            )
+
+        two_bytes = pick_bytes("two_bytes", l_two)
+        wb_mx = mx_tiles("wb", H)
+        wb_woven = [tile("wb_woven%d" % u, [P, HALF, SLOTS], BF16) for u in range(2)]
+        weave(nc.scalar.copy, wb_woven[0][:], wb_raw[:, :, halves[0]])
+        weave(nc.vector.tensor_copy, wb_woven[1][:], wb_raw[:, :, halves[1]])
+        offs_bytes = pick_bytes("offs_bytes", l_offs)
+        quantise_into(wb_mx, halves[1], wb_woven[1])
+        quantise_into(wb_mx, halves[0], wb_woven[0])
+        two_mx = (pick_words("two_words", l_two), two_bytes)
+        offs_mx = (pick_words("offs_words", l_offs), offs_bytes)
 
         d_win = []
-        for t in range(4):
-            acc = ps.tile([P, H], F32, name="acc_d%d" % t, tag="bank%d" % t)
-            product(acc[:], two_w[:, blocks[t]], two_s[:, blocks[t]], wb_c[:], wb_s[:])
+        for t in range(SLOTS):
+            acc = bank("d_acc%d" % t, H, t)
+            product(acc[:], two_mx, t, wb_mx)
             win = tile("d_win%d" % t, [P, 2 * H], F32)
-            nc.gpsimd.memset(win[:, H:], 0.0)
+            nc.vector.memset(win[:, H:], 0.0)
             nc.scalar.activation(win[:, :H], acc[:], ACT.Copy, scale=mag[:, t : t + 1])
             d_win.append(win)
-        wa_w = weave(nc.scalar.copy, "wa_w", wa_raw[:], H)
+        wa_woven = tile("wa_woven", [P, H, SLOTS], BF16)
+        weave(nc.scalar.copy, wa_woven[:], wa_raw[:])
 
-        hi = tile("hi", [P, 4, H], BF16)
-        for t in range(4):
-            nc.vector.tensor_copy(hi[:, t, :], d_win[t][:].indirect(l_n2[:]))
-        wa_c = tile("wa_c", [P, H], U32)
-        wa_s = tile("wa_s", [P, H], U8)
-        quantise(wa_w, wa_c[:], wa_s[:])
-        lo = tile("lo", [P, 4, H], BF16, tag="wa_w")
-        for t in range(4):
-            nc.vector.tensor_copy(lo[:, t, :], d_win[t][:].indirect(l_n3[:]))
+        upper = tile("upper", [P, SLOTS, H], BF16)
+        for t in range(SLOTS):
+            nc.vector.tensor_copy(upper[:, t, :], d_win[t][:].indirect(l_n2[:]))
+        wa_mx = quantise("wa", wa_woven, H)
+        lower = tile("lower", [P, SLOTS, H], BF16, tag="wa_woven")
+        for t in range(SLOTS):
+            nc.vector.tensor_copy(lower[:, t, :], d_win[t][:].indirect(l_n3[:]))
 
-        w1_b = tile("w1_b", [P, 4, N], BF16)
-        for j in range(4):
+        w1_signed = tile("w1_signed", [P, SLOTS, N], BF16)
+        for t in range(SLOTS):
             nc.scalar.activation(
-                w1_b[:, j, :].rearrange("p (t c e) -> p t c e", t=4, e=4),
-                w1_raw[:, j, :].rearrange("p (c t e) -> p t c e", t=4, e=4),
+                w1_signed[:, t, :].rearrange("p (s c e) -> p s c e", s=SLOTS, e=RUN),
+                w1_raw[:, t, :].rearrange("p (c s e) -> p s c e", s=SLOTS, e=RUN),
                 ACT.Copy,
-                scale=sign[:, j : j + 1],
+                scale=sign[:, t : t + 1],
             )
-        w1_w = tile("w1_w", [P, N, 4], BF16)
-
-        def weave_w1(ms):
-            nc.scalar.copy(
-                w1_w[:, ms, :].rearrange("p (c i) j -> p c j i", i=4),
-                w1_b[:, :, ms].rearrange("p j (c i) -> p c j i", i=4),
-            )
-
-        weave_w1(halves[0])
+        w1_woven = tile("w1_woven", [P, N, SLOTS], BF16)
+        weave(nc.scalar.copy, w1_woven[:, halves[0], :], w1_signed[:, :, halves[0]])
 
         y_acc = []
         y_win = []
-        y_sb = [[tile("y_sb%d_%d" % (u, t), [P, HALF], F32) for t in range(4)] for u in range(2)]
-        a32 = [tile("a32_%d" % u, [P, 4, HALF], F32) for u in range(2)]
+        centred = [tile("centred%d" % u, [P, SLOTS, HALF], F32) for u in range(2)]
 
-        def fetch_y(u, t):
-            nc.scalar.activation(y_sb[u][t][:], y_acc[t][:, halves[u]], ACT.Copy, scale=mag[:, t : t + 1])
-            nc.vector.tensor_tensor(a32[u][:, t, :], y_win[t][:].indirect(l_n1[:, lcols[u]]), y_sb[u][t][:], ALU.add)
+        def centre(u, t):
+            plain = tile("y_plain%d_%d" % (u, t), [P, HALF], F32)
+            nc.scalar.activation(plain[:], y_acc[t][:, halves[u]], ACT.Copy, scale=mag[:, t : t + 1])
+            nc.vector.tensor_tensor(centred[u][:, t, :], y_win[t][:].indirect(l_n1[:, list_halves[u]]), plain[:], ALU.add)
 
-        for t in range(4):
-            acc = ps.tile([P, H], F32, name="acc_y%d" % t, tag="bank%d" % (4 + t))
-            product(acc[:], offs_w[:, blocks[t]], offs_s[:, blocks[t]], wa_c[:], wa_s[:])
+        def cap(u):
+            rounded = tile("rounded%d" % u, [P, SLOTS, HALF], BF16)
+            nc.scalar.copy(rounded[:], centred[u][:])
+            capped = tile("capped%d" % u, [P, SLOTS, HALF], BF16)
+            nc.vector.tensor_tensor(capped[:], rounded[:], upper[:, :, halves[u]], ALU.min)
+            return capped
+
+        def floor(u, capped, tag):
+            z = tile("z%d" % u, [P, SLOTS, HALF], BF16, tag=tag)
+            nc.vector.tensor_tensor(z[:], capped[:], lower[:, :, halves[u]], ALU.max)
+            return z
+
+        for t in range(SLOTS):
+            acc = bank("y_acc%d" % t, H, SLOTS + t)
+            product(acc[:], offs_mx, t, wa_mx)
             win = tile("y_win%d" % t, [P, H], F32)
-            nc.scalar.activation(win[:], acc[:], ACT.Copy, scale=nhalf[:, t : t + 1])
+            nc.scalar.activation(win[:], acc[:], ACT.Copy, scale=neg_half_mag[:, t : t + 1])
             y_acc.append(acc)
             y_win.append(win)
-            fetch_y(0, t)
-        fetch_y(1, 0)
-        fetch_y(1, 1)
-        a16 = tile("a16", [P, 4, HALF], BF16)
-        nc.scalar.copy(a16[:], a32[0][:])
-        low0 = tile("low0", [P, 4, HALF], BF16)
-        nc.vector.tensor_tensor(low0[:], a16[:], hi[:, :, halves[0]], ALU.min)
-        fetch_y(1, 2)
-        z0 = tile("z0", [P, 4, HALF], BF16)
-        nc.vector.tensor_tensor(z0[:], low0[:], lo[:, :, halves[0]], ALU.max)
-        fetch_y(1, 3)
-        weave_w1(halves[1])
-        z_w0 = weave(nc.scalar.copy, "z_w0", z0[:], HALF)
-        w1_c = tile("w1_c", [P, N], U32)
-        w1_s = tile("w1_s", [P, N], U8)
-        quantise(w1_w[:].rearrange("p m j -> p (m j)"), w1_c[:], w1_s[:])
-        low1 = tile("low1", [P, 4, HALF], BF16)
-        b16 = tile("b16", [P, 4, HALF], BF16)
-        nc.scalar.copy(b16[:], a32[1][:])
-        nc.vector.tensor_tensor(low1[:], b16[:], hi[:, :, halves[1]], ALU.min)
-        z_c = [tile("z_c%d" % u, [P, HALF], U32) for u in range(2)]
-        z_s = [tile("z_s%d" % u, [P, HALF], U8) for u in range(2)]
-        quantise(z_w0, z_c[0][:], z_s[0][:])
-        z1 = tile("z1", [P, 4, HALF], BF16, tag="z_w0")
-        nc.vector.tensor_tensor(z1[:], low1[:], lo[:, :, halves[1]], ALU.max)
-        z_w1 = weave(nc.scalar.copy, "z_w1", z1[:], HALF)
-        quantise(z_w1, z_c[1][:], z_s[1][:])
+            centre(0, t)
 
-        h_acc = [ps.tile([P, H], F32, name="acc_h%d" % t, tag="bank%d" % t) for t in range(4)]
-        rl = [tile("rl%d" % t, [P, H], F32, tag="z_w0" if t == 2 else None) for t in range(4)]
+        centre(1, 0)
+        centre(1, 1)
+        capped0 = cap(0)
+        centre(1, 2)
+        z0 = floor(0, capped0, None)
+        centre(1, 3)
+        weave(nc.scalar.copy, w1_woven[:, halves[1], :], w1_signed[:, :, halves[1]])
+        z0_woven = tile("z0_woven", [P, HALF, SLOTS], BF16)
+        weave(nc.scalar.copy, z0_woven[:], z0[:])
+        w1_mx = quantise("w1", w1_woven, N)
+        capped1 = cap(1)
+        z_mx = [quantise("z0", z0_woven, HALF)]
+        z1 = floor(1, capped1, "z0_woven")
+        z1_woven = tile("z1_woven", [P, HALF, SLOTS], BF16)
+        weave(nc.scalar.copy, z1_woven[:], z1[:])
+        z_mx.append(quantise("z1", z1_woven, HALF))
+
+        h_acc = [bank("h_acc%d" % t, H, t) for t in range(SLOTS)]
+        rl = [tile("rl%d" % t, [P, H], F32, tag="z0_woven" if t == LAST - 1 else None) for t in range(SLOTS)]
         for u in range(2):
-            for t in range(4):
-                product(h_acc[t][:, halves[u]], w1_c[:, blocks[t]], w1_s[:, blocks[t]], z_c[u][:], z_s[u][:])
+            for t in range(SLOTS):
+                product(h_acc[t][:, halves[u]], w1_mx, t, z_mx[u])
                 nc.scalar.activation(rl[t][:, halves[u]], h_acc[t][:, halves[u]], ACT.Relu)
 
-        out_rows = out.rearrange("(c t e) n -> t c e n", t=4, e=4)
-        for t in range(4):
-            if t < SPLIT:
-                ds = tile("ds%d" % t, [P, H], F32)
-                for u in range(2):
-                    nc.vector.tensor_copy(ds[:].indirect(l_n4[:, lcols[u]]), rl[t][:, halves[u]])
-            else:
-                ds = tile("ds%d" % t, [P, 2 * H], F32)
-                nc.vector.tensor_copy(ds[:].indirect(l_n4[:]), rl[t][:])
+        out_slots = out.rearrange("(c t e) n -> t c e n", t=SLOTS, e=RUN)
+        for t in range(LAST):
+            ds = tile("ds%d" % t, [P, H], F32)
+            for u in range(2):
+                nc.vector.tensor_copy(ds[:].indirect(l_n4[:, list_halves[u]]), rl[t][:, halves[u]])
             res = tile("res%d" % t, [P, H], F32)
-            if t < ON_PE:
-                nh = tile("nh%d" % t, [P, H], F32)
-                nc.scalar.activation(nh[:], h_acc[t][:], ACT.Copy, scale=-0.5)
-                for u in range(2):
-                    turned = ps.tile([P, HALF], F32, name="turned%d_%d" % (t, u), tag="bank%d" % (4 + u))
-                    for k in range(2):
-                        b = blocks[2 * u + k]
-                        nc.tensor.matmul(turned[:, blocks[k]], nh[:, b], ident[:], start=True, stop=False, is_transpose=True)
-                        nc.tensor.matmul(turned[:, blocks[k]], ds[:, b], ident[:], start=False, stop=True, is_transpose=True)
-                    turned_sb = tile("turned_sb%d_%d" % (t, u), [P, HALF], F32)
-                    nc.scalar.copy(turned_sb[:], turned[:])
-                    back = ps.tile([P, HALF], F32, name="back%d_%d" % (t, u), tag="bank%d" % (6 + u))
-                    for k in range(2):
-                        nc.tensor.transpose(back[:, blocks[k]], turned_sb[:, blocks[k]], ident[:])
-                    nc.scalar.copy(res[:, halves[u]], back[:])
-            else:
-                nc.vector.scalar_tensor_tensor(res[:], h_acc[t][:], -0.5, ds[:, :H], ALU.mult, ALU.add)
-            nc.sync.dma_start(out_rows[t], res[:])
+            neg_half_h = tile("neg_half_h%d" % t, [P, H], F32)
+            nc.scalar.activation(neg_half_h[:], h_acc[t][:], ACT.Copy, scale=-0.5)
+            for u in range(2):
+                turned = bank("turned%d_%d" % (t, u), HALF, SLOTS + u)
+                for b in range(2):
+                    cols = blocks[2 * u + b]
+                    nc.tensor.matmul(turned[:, blocks[b]], neg_half_h[:, cols], ident[:], start=True, stop=False, is_transpose=True)
+                    nc.tensor.matmul(turned[:, blocks[b]], ds[:, cols], ident[:], start=False, stop=True, is_transpose=True)
+                turned_sb = tile("turned_sb%d_%d" % (t, u), [P, HALF], F32)
+                nc.scalar.copy(turned_sb[:], turned[:])
+                back = bank("back%d_%d" % (t, u), HALF, SLOTS + 2 + u)
+                for b in range(2):
+                    nc.tensor.transpose(back[:, blocks[b]], turned_sb[:, blocks[b]], ident[:])
+                nc.scalar.copy(res[:, halves[u]], back[:])
+            nc.sync.dma_start(out_slots[t], res[:])
+
+        ds = tile("ds%d" % LAST, [P, 2 * H], F32)
+        nc.vector.tensor_copy(ds[:].indirect(l_n4[:]), rl[LAST][:])
+        for u in range(2):
+            res = tile("res%d_%d" % (LAST, u), [P, HALF], F32)
+            nc.vector.scalar_tensor_tensor(res[:], h_acc[LAST][:, halves[u]], -0.5, ds[:, halves[u]], ALU.mult, ALU.add)
+            nc.sync.dma_start(out_slots[LAST][:, :, halves[u]], res[:])

from contextlib import ExitStack

import concourse.mybir as mybir
from concourse.masks import make_identity

K, T, S, N, H = 512, 2048, 512, 512, 512
FLOPS = 2 * (2 * K * S * H) + 2 * S * N * H

F32 = mybir.dt.float32
BF16 = mybir.dt.bfloat16
I32 = mybir.dt.int32
U32 = mybir.dt.uint32
U16 = mybir.dt.uint16
U8 = mybir.dt.uint8
FP8X4 = mybir.dt.float8_e4m3fn_x4
ALU = mybir.AluOpType
ACT = mybir.ActivationFunctionType

P = 128
SLOTS = 4
RUN = 4
LIST_COLS = S // 16
HALF = H // 2
QUADRANT = 32
LAST = SLOTS - 1


def tile_picked_twtclampbsend_none_p_kernel(
    tc, x_words, x_scales, wa, wb, gt, w1, offs, two, n1, n2, n3, n4, out
):
    nc = tc.nc
    with ExitStack() as ctx:
        sb = ctx.enter_context(tc.tile_pool(name="sb", bufs=1))
        ps = ctx.enter_context(tc.psum_pool(name="ps", bufs=1))

        def tile(name, shape, dtype, tag=None):
            return sb.tile(shape, dtype, name=name, tag=tag or name, align_bytes=64)

        def bank(name, width, number):
            return ps.tile([P, width], F32, name=name, tag="bank%d" % number)

        def load_list(name, src):
            lst = tile(name, [P, LIST_COLS], U16)
            nc.sync.dma_start(lst[:], src)
            return lst

        def load_weight(name, src):
            raw = tile(name, [P, SLOTS, H], F32)
            nc.sync.dma_start(raw[:], src.rearrange("(p r) n -> p r n", r=SLOTS))
            return raw

        halves = [slice(0, HALF), slice(HALF, H)]
        list_halves = [slice(0, LIST_COLS // 2), slice(LIST_COLS // 2, LIST_COLS)]
        blocks = [slice(P * t, P * t + P) for t in range(SLOTS)]

        xs = tile("xs", [P, T], U8)
        l_two = load_list("l_two", two)
        for q in range(P // QUADRANT):
            nc.sync.dma_start(
                xs[QUADRANT * q : QUADRANT * (q + 1), :].bitcast(I32),
                x_scales[0, 4 * q : 4 * q + 4, :].bitcast(I32).partition_broadcast(QUADRANT // 4),
            )
        wb_raw = load_weight("wb_raw", wb)
        l_offs = load_list("l_offs", offs)
        xw = tile("xw", [P, T], U32)
        nc.sync.dma_start(xw[:].bitcast(I32), x_words[0].rearrange("p n r -> p (n r)").bitcast(I32))
        gate = tile("gate", [P, SLOTS], F32)
        with nc.allow_non_contiguous_dma(reason="one gate value a row"):
            for e in range(RUN):
                nc.sync.dma_start(gate[e:P:RUN, :], gt.rearrange("(c t e) o -> e c (t o)", t=SLOTS, e=RUN)[e])
        l_n2 = load_list("l_n2", n2)
        l_n3 = load_list("l_n3", n3)
        wa_raw = load_weight("wa_raw", wa)
        l_n1 = load_list("l_n1", n1)
        w1_raw = tile("w1_raw", [P, SLOTS, N], F32)
        for t in range(SLOTS):
            nc.sync.dma_start(w1_raw[:, t, :], w1.rearrange("(c t e) n -> t c e n", t=SLOTS, e=RUN)[t])
        l_n4 = load_list("l_n4", n4)

        ident = tile("ident", [P, P], F32)
        make_identity(nc, ident[:])
        twice = tile("twice", [P, SLOTS], F32)
        sign = tile("sign", [P, SLOTS], F32)
        mag = tile("mag", [P, SLOTS], F32)
        neg_half_mag = tile("neg_half_mag", [P, SLOTS], F32)
        nc.gpsimd.tensor_scalar(twice[:], gate[:], 0.0, 2.0, ALU.is_ge, ALU.mult)
        nc.gpsimd.tensor_scalar(sign[:], twice[:], 1.0, -1.0, ALU.mult, ALU.add)
        nc.scalar.activation(mag[:], gate[:], ACT.Abs)
        nc.scalar.activation(neg_half_mag[:], mag[:], ACT.Copy, scale=-0.5)

        def pick_bytes(name, lst):
            picked = tile(name + "_picked", [P, S], U8)
            nc.vector.tensor_copy(picked[:], xs[:].indirect(lst[:]))
            dealt = tile(name, [P, S], U8)
            nc.vector.tensor_copy(
                dealt[:].bitcast(I32).rearrange("p (t c) -> p t c", t=SLOTS),
                picked[:].bitcast(I32).rearrange("p (c t) -> p t c", t=SLOTS),
            )
            return dealt

        def pick_words(name, lst):
            dealt = tile(name, [P, S], U32)
            nc.vector.tensor_copy(dealt[:].rearrange("p (t c e) -> p c t e", t=SLOTS, e=RUN), xw[:].indirect(lst[:]))
            return dealt

        def weave(copy, woven, planes):
            copy(woven.rearrange("p (a i) r -> p a r i", i=4), planes.rearrange("p r (a i) -> p a r i", i=4))

        def mx_tiles(name, width):
            return tile(name + "_codes", [P, width], U32), tile(name + "_scales", [P, width], U8)

        def quantise_into(operand, cols, woven):
            nc.vector.quantize_mx(
                out=operand[0][:, cols].bitcast(FP8X4),
                scales=operand[1][:, cols],
                in_=woven[:].rearrange("p n r -> p (n r)"),
            )

        def quantise(name, woven, width):
            operand = mx_tiles(name, width)
            quantise_into(operand, slice(0, width), woven)
            return operand

        def product(acc, stationary, t, moving):
            nc.tensor.matmul_mx(
                out=acc,
                lhsT=stationary[0][:, blocks[t]].bitcast(FP8X4),
                lhsT_scale=stationary[1][:, blocks[t]],
                rhs=moving[0][:].bitcast(FP8X4),
                rhs_scale=moving[1][:],
                start=True,
                stop=True,
            )

        two_bytes = pick_bytes("two_bytes", l_two)
        wb_mx = mx_tiles("wb", H)
        wb_woven = [tile("wb_woven%d" % u, [P, HALF, SLOTS], BF16) for u in range(2)]
        weave(nc.scalar.copy, wb_woven[0][:], wb_raw[:, :, halves[0]])
        weave(nc.vector.tensor_copy, wb_woven[1][:], wb_raw[:, :, halves[1]])
        offs_bytes = pick_bytes("offs_bytes", l_offs)
        quantise_into(wb_mx, halves[1], wb_woven[1])
        quantise_into(wb_mx, halves[0], wb_woven[0])
        two_mx = (pick_words("two_words", l_two), two_bytes)
        offs_mx = (pick_words("offs_words", l_offs), offs_bytes)

        d_win = []
        for t in range(SLOTS):
            acc = bank("d_acc%d" % t, H, t)
            product(acc[:], two_mx, t, wb_mx)
            win = tile("d_win%d" % t, [P, 2 * H], F32)
            nc.vector.memset(win[:, H:], 0.0)
            nc.scalar.activation(win[:, :H], acc[:], ACT.Copy, scale=mag[:, t : t + 1])
            d_win.append(win)
        wa_woven = tile("wa_woven", [P, H, SLOTS], BF16)
        weave(nc.scalar.copy, wa_woven[:], wa_raw[:])

        upper = tile("upper", [P, SLOTS, H], BF16)
        for t in range(SLOTS):
            nc.vector.tensor_copy(upper[:, t, :], d_win[t][:].indirect(l_n2[:]))
        wa_mx = quantise("wa", wa_woven, H)
        lower = tile("lower", [P, SLOTS, H], BF16, tag="wa_woven")
        for t in range(SLOTS):
            nc.vector.tensor_copy(lower[:, t, :], d_win[t][:].indirect(l_n3[:]))

        w1_signed = tile("w1_signed", [P, SLOTS, N], BF16)
        for t in range(SLOTS):
            nc.scalar.activation(
                w1_signed[:, t, :].rearrange("p (s c e) -> p s c e", s=SLOTS, e=RUN),
                w1_raw[:, t, :].rearrange("p (c s e) -> p s c e", s=SLOTS, e=RUN),
                ACT.Copy,
                scale=sign[:, t : t + 1],
            )
        w1_woven = tile("w1_woven", [P, N, SLOTS], BF16)
        weave(nc.scalar.copy, w1_woven[:, halves[0], :], w1_signed[:, :, halves[0]])

        y_acc = []
        y_win = []
        centred = [tile("centred%d" % u, [P, SLOTS, HALF], F32) for u in range(2)]

        def centre(u, t):
            plain = tile("y_plain%d_%d" % (u, t), [P, HALF], F32)
            nc.scalar.activation(plain[:], y_acc[t][:, halves[u]], ACT.Copy, scale=mag[:, t : t + 1])
            nc.vector.tensor_tensor(centred[u][:, t, :], y_win[t][:].indirect(l_n1[:, list_halves[u]]), plain[:], ALU.add)

        def cap(u):
            rounded = tile("rounded%d" % u, [P, SLOTS, HALF], BF16)
            nc.scalar.copy(rounded[:], centred[u][:])
            capped = tile("capped%d" % u, [P, SLOTS, HALF], BF16)
            nc.vector.tensor_tensor(capped[:], rounded[:], upper[:, :, halves[u]], ALU.min)
            return capped

        def floor(u, capped, tag):
            z = tile("z%d" % u, [P, SLOTS, HALF], BF16, tag=tag)
            nc.vector.tensor_tensor(z[:], capped[:], lower[:, :, halves[u]], ALU.max)
            return z

        for t in range(SLOTS):
            acc = bank("y_acc%d" % t, H, SLOTS + t)
            product(acc[:], offs_mx, t, wa_mx)
            win = tile("y_win%d" % t, [P, H], F32)
            nc.scalar.activation(win[:], acc[:], ACT.Copy, scale=neg_half_mag[:, t : t + 1])
            y_acc.append(acc)
            y_win.append(win)
            centre(0, t)

        centre(1, 0)
        centre(1, 1)
        capped0 = cap(0)
        centre(1, 2)
        z0 = floor(0, capped0, None)
        centre(1, 3)
        weave(nc.scalar.copy, w1_woven[:, halves[1], :], w1_signed[:, :, halves[1]])
        z0_woven = tile("z0_woven", [P, HALF, SLOTS], BF16)
        weave(nc.scalar.copy, z0_woven[:], z0[:])
        w1_mx = quantise("w1", w1_woven, N)
        capped1 = cap(1)
        z_mx = [quantise("z0", z0_woven, HALF)]
        z1 = floor(1, capped1, "z0_woven")
        z1_woven = tile("z1_woven", [P, HALF, SLOTS], BF16)
        weave(nc.scalar.copy, z1_woven[:], z1[:])
        z_mx.append(quantise("z1", z1_woven, HALF))

        h_acc = [bank("h_acc%d" % t, H, t) for t in range(SLOTS)]
        rl = [tile("rl%d" % t, [P, H], F32, tag="z0_woven" if t == LAST - 1 else None) for t in range(SLOTS)]
        for u in range(2):
            for t in range(SLOTS):
                product(h_acc[t][:, halves[u]], w1_mx, t, z_mx[u])
                nc.scalar.activation(rl[t][:, halves[u]], h_acc[t][:, halves[u]], ACT.Relu)

        out_slots = out.rearrange("(c t e) n -> t c e n", t=SLOTS, e=RUN)
        for t in range(LAST):
            ds = tile("ds%d" % t, [P, H], F32)
            for u in range(2):
                nc.vector.tensor_copy(ds[:].indirect(l_n4[:, list_halves[u]]), rl[t][:, halves[u]])
            res = tile("res%d" % t, [P, H], F32)
            neg_half_h = tile("neg_half_h%d" % t, [P, H], F32)
            nc.scalar.activation(neg_half_h[:], h_acc[t][:], ACT.Copy, scale=-0.5)
            for u in range(2):
                turned = bank("turned%d_%d" % (t, u), HALF, SLOTS + u)
                for b in range(2):
                    cols = blocks[2 * u + b]
                    nc.tensor.matmul(turned[:, blocks[b]], neg_half_h[:, cols], ident[:], start=True, stop=False, is_transpose=True)
                    nc.tensor.matmul(turned[:, blocks[b]], ds[:, cols], ident[:], start=False, stop=True, is_transpose=True)
                turned_sb = tile("turned_sb%d_%d" % (t, u), [P, HALF], F32)
                nc.scalar.copy(turned_sb[:], turned[:])
                back = bank("back%d_%d" % (t, u), HALF, SLOTS + 2 + u)
                for b in range(2):
                    nc.tensor.transpose(back[:, blocks[b]], turned_sb[:, blocks[b]], ident[:])
                nc.scalar.copy(res[:, halves[u]], back[:])
            nc.sync.dma_start(out_slots[t], res[:])

        ds = tile("ds%d" % LAST, [P, 2 * H], F32)
        nc.vector.tensor_copy(ds[:].indirect(l_n4[:]), rl[LAST][:])
        for u in range(2):
            res = tile("res%d_%d" % (LAST, u), [P, HALF], F32)
            nc.vector.scalar_tensor_tensor(res[:], h_acc[LAST][:, halves[u]], -0.5, ds[:, halves[u]], ALU.mult, ALU.add)
            nc.sync.dma_start(out_slots[LAST][:, :, halves[u]], res[:])
